import numpy as np
import ml_dtypes


def mxq(x, axis, fmt="e4m3"):
    dtype, down = {"e4m3": (ml_dtypes.float8_e4m3fn, 7), "e5m2": (ml_dtypes.float8_e5m2, 14)}[fmt]
    v = np.moveaxis(np.asarray(x, np.float32).astype(ml_dtypes.bfloat16).astype(np.float64), axis, -1)
    blocks = v.reshape(v.shape[:-1] + (-1, 32))
    amax = np.abs(blocks).max(-1, keepdims=True)
    byte = np.maximum(np.where(amax > 0, np.frexp(amax)[1] - 1 + 127, 0) - down, 1)
    scale = np.exp2(byte - 127.0)
    codes = (blocks / scale).astype(np.float32).astype(dtype).astype(np.float64)
    return np.moveaxis((codes * scale).reshape(v.shape), -1, axis)


WIDE = False


def mx_kscale(k):
    if not WIDE:
        return np.ones(k)
    levels = np.array([10, -10, 5, -5, 0])
    if k % 512:
        return np.exp2(np.random.permutation(np.resize(levels, k // 32))).repeat(32)
    a = np.empty((k // 512, 16))
    for p in range(k // 512):
        a[p, :8] = np.random.permutation(np.resize(levels, 8))
        for g in range(8):
            far = levels[np.abs(levels - a[p, g]) >= 10]
            a[p, g + 8] = far[np.random.randint(len(far))]
    return np.exp2(a.ravel()).repeat(32)


def f64(x):
    return np.asarray(x).astype(np.float64)


def striped(idx):
    return np.tile(idx.reshape(-1, 16).T, (8, 1)).astype(np.uint16)


def unstriped(offs):
    return offs[:16].T.reshape(-1).astype(np.int64)


def striped8(idx):
    return np.concatenate([x.reshape(-1, 16).T for x in idx]).astype(np.uint16)


def runs(offs, k):
    lists = np.stack([offs[16 * r : 16 * r + 16].T.reshape(-1) for r in range(8)]).astype(np.int64)
    return lists[np.arange(k) % 512 // 64]


def pack_weight(w):
    k, n = w.shape
    w = f64(np.asarray(w, np.float32).astype(ml_dtypes.bfloat16)).reshape(k // 32, 32, n)
    amax = np.abs(w).max(1)
    byte = np.clip(np.where(amax > 0, np.frexp(amax)[1] - 1 + 127 - 7, 1), 1, 254)
    scaled = (w * np.exp2(127.0 - byte)[:, None, :]).reshape(k, n).astype(np.float32)
    words = np.ascontiguousarray(scaled.reshape(k // 512, 128, 4, n).transpose(0, 1, 3, 2)).astype(ml_dtypes.float8_e4m3fn).view(np.uint8)
    return words, np.ascontiguousarray(byte.astype(np.uint8).reshape(k // 512, 16, n))


def unpack_weight(words, scales):
    g, p, n, _ = words.shape
    vals = np.ascontiguousarray(words).view(ml_dtypes.float8_e4m3fn).astype(np.float64) * np.repeat(np.exp2(scales.astype(np.float64) - 127.0), 8, axis=1)[..., None]
    return vals.transpose(0, 1, 3, 2).reshape(g * 512, n)

def planes(y):
    n, m = y.shape
    v = y.astype(np.float32).astype(ml_dtypes.bfloat16).astype(np.float64).reshape(n // 32, 32, m)
    top = np.abs(v).max(1)
    byte = np.clip(np.where(top > 0, np.frexp(top)[1] - 1 + 127 - 7, 1), 1, 254)
    codes = (v * np.exp2(127.0 - byte)[:, None, :]).reshape(n, m).astype(np.float32).astype(ml_dtypes.float8_e4m3fn).view(np.uint8)
    words = codes.reshape(n // 512, 128, 4, m).transpose(0, 1, 3, 2)
    return np.ascontiguousarray(words), np.ascontiguousarray(byte.astype(np.uint8).reshape(n // 512, 16, m))


K, T, S, N, G, H = 512, 2048, 512, 512, 2048, 512


def setup_inputs():
    n = np.random.standard_normal
    s = mx_kscale(K)[:, None]
    u = mx_kscale(S)
    packed_xT = pack_weight(n((K, T)) * s)
    packed_dT = pack_weight(n((K, G)) / s)
    packed_w1 = pack_weight(n((H, N)) / np.sqrt(H) / u[:, None])
    return {
        "x_words": packed_xT[0],
        "x_scales": packed_xT[1],
        "d_words": packed_dT[0],
        "d_scales": packed_dT[1],
        "gn": (np.random.uniform(0.5, 1.5, (H, 1)) * u[:, None]).astype(np.float32),
        "w1_words": packed_w1[0],
        "w1_scales": packed_w1[1],
        "offs": striped(np.random.permutation(T)[:S]),
        "kidx": striped8(np.random.randint(0, G, (8, H))),
        "n1": striped8(np.stack([np.random.permutation(S) for _ in range(8)])),
        "n2": striped8(np.stack([np.random.permutation(S) for _ in range(8)])),
        "n3": striped8(np.stack([np.random.permutation(S) for _ in range(8)])),
        "n4": striped8(np.stack([np.random.permutation(S) for _ in range(8)])),
        "n5": striped8(np.stack([np.random.permutation(S) for _ in range(8)])),
    }


def reference(x_words, x_scales, d_words, d_scales, gn, w1_words, w1_scales, offs, kidx, n1, n2, n3, n4, n5):
    d_kidx = unpack_weight(d_words, d_scales)[np.arange(K)[:, None], runs(kidx, K)]
    xq = unpack_weight(x_words, x_scales)[:, unstriped(offs)]
    s = 0.0625 * (d_kidx.T @ xq)
    z = f64(gn) * (0.75 * (s * (s[np.arange(H)[:, None], runs(n1, H)]) + (s[np.arange(H)[:, None], runs(n2, H)]) * (s[np.arange(H)[:, None], runs(n3, H)])))
    h = unpack_weight(w1_words, w1_scales).T @ mxq(z, 0, "e4m3")
    sq = (h) ** 2
    out_0 = (h[np.arange(N)[:, None], runs(n5, N)]) / (np.sqrt(sq + sq[np.arange(N)[:, None], runs(n4, N)] + 0.25))
    return (out_0,) + planes(out_0)

@@ -1,0 +1,310 @@
+from contextlib import ExitStack
+
+import concourse.mybir as mybir
+
+F32 = mybir.dt.float32
+BF16 = mybir.dt.bfloat16
+I32 = mybir.dt.int32
+U32 = mybir.dt.uint32
+U16 = mybir.dt.uint16
+U8 = mybir.dt.uint8
+FP8X4 = mybir.dt.float8_e4m3fn_x4
+ACT = mybir.ActivationFunctionType
+ALU = mybir.AluOpType
+
+P = 128
+PACK = 4
+TABLE = 2048
+S = 512
+HALF = 256
+FLOPS = 2 * 2 * 512 * 512 * 512
+
+
+def tile_picked_keydotrms_none_po_kernel(
+    tc, x_words, x_scales, d_words, d_scales, gn, w1_words, w1_scales,
+    offs, kidx, n1, n2, n3, n4, n5, out_0, out_1, out_2,
+):
+    nc = tc.nc
+    halves = [slice(c * HALF, (c + 1) * HALF) for c in range(2)]
+    entries = [slice(c * HALF // 16, (c + 1) * HALF // 16) for c in range(2)]
+
+    with ExitStack() as ctx:
+        lists = ctx.enter_context(tc.tile_pool(name="lists", bufs=1))
+        keep = ctx.enter_context(tc.tile_pool(name="keep", bufs=1))
+        psum = ctx.enter_context(tc.psum_pool(name="psum", bufs=1))
+
+        def sb(name, shape, dtype, tag=None):
+            return keep.tile(shape, dtype, name=name, tag=tag or name, align_bytes=64)
+
+        def load_list(name, src):
+            tile = lists.tile([P, S // 16], U16, name=name)
+            nc.sync.dma_start(tile[:], src)
+            return tile
+
+        def words_view(src):
+            return src[0].rearrange("p n t -> p (n t)").bitcast(I32)
+
+        def load_scale_rows(tile, src):
+            rows = src[0].bitcast(I32)
+            nc.sync.dma_start(
+                tile[:].bitcast(I32), rows.unsqueeze(1).to_broadcast([16, 8, rows.shape[1]])
+            )
+
+        def deal(ap):
+            return ap.rearrange("p (m t) -> p t m", t=PACK)
+
+        def dealt(ap):
+            return ap.rearrange("p (t m) -> p t m", t=PACK)
+
+        def settle_scale_rows(queue, tile):
+            for r in range(1, 4):
+                queue.dma_start(tile[r:P:32, :].bitcast(I32), tile[8 * r : P : 32, :].bitcast(I32))
+
+        d_byte_table = sb("d_byte_table", [P, TABLE], U8)
+        x_byte_table = sb("x_byte_table", [P, TABLE], U8)
+        d_word_table = sb("d_word_table", [P, TABLE], U32)
+        x_word_table = sb("x_word_table", [P, TABLE], U32)
+        w_bytes_raw = sb("w_bytes_raw", [P, S], U8)
+        w_words_raw = sb("w_words_raw", [P, S], U32)
+        gn_sb = sb("gn_sb", [P, PACK], F32)
+
+        kidx_sb = load_list("kidx_sb", kidx)
+        load_scale_rows(d_byte_table, d_scales)
+        offs_sb = load_list("offs_sb", offs)
+        load_scale_rows(x_byte_table, x_scales)
+        nc.sync.dma_start(gn_sb[:], gn.rearrange("(p t) o -> p (t o)", t=PACK))
+        nc.sync.dma_start(d_word_table[:].bitcast(I32), words_view(d_words))
+        n1_sb = load_list("n1_sb", n1)
+        n2_sb = load_list("n2_sb", n2)
+        n3_sb = load_list("n3_sb", n3)
+        nc.sync.dma_start(x_word_table[:].bitcast(I32), words_view(x_words))
+        n4_sb = load_list("n4_sb", n4)
+        n5_sb = load_list("n5_sb", n5)
+        nc.sync.dma_start(w_words_raw[:].bitcast(I32), words_view(w1_words))
+        load_scale_rows(w_bytes_raw, w1_scales)
+
+        d_bytes_picked = sb("d_bytes_picked", [P, S], U8)
+        x_bytes_picked = sb("x_bytes_picked", [P, S], U8)
+        dx_bytes = sb("dx_bytes", [P, 2 * S], U8)
+        d_bytes = dx_bytes[:, :S]
+        x_bytes = dx_bytes[:, S:]
+        gain = sb("gain", [P, PACK], F32)
+
+        nc.scalar.activation(gain[:], gn_sb[:], ACT.Copy, scale=0.75 * 0.0625)
+        nc.vector.tensor_copy(d_bytes_picked[:], d_byte_table[:].indirect(kidx_sb[:]))
+        nc.vector.tensor_copy(x_bytes_picked[:], x_byte_table[:].indirect(offs_sb[:]))
+        nc.vector.tensor_copy(dealt(d_bytes), deal(d_bytes_picked[:]))
+        nc.vector.tensor_copy(x_bytes.bitcast(I32), x_bytes_picked[:].bitcast(I32))
+        settle_scale_rows(nc.scalar, dx_bytes)
+        d_words_picked = sb("d_words_picked", [P, S], U32)
+        d_codes = sb("d_codes", [P, S], U32)
+        nc.vector.tensor_copy(d_words_picked[:], d_word_table[:].indirect(kidx_sb[:]))
+        nc.vector.tensor_copy(dealt(d_codes[:]), deal(d_words_picked[:]))
+        x_codes = sb("x_codes", [P, S], U32)
+
+        def product(bank, lhs_codes, lhs_bytes, rhs_codes, rhs_bytes, t):
+            rows = slice(t * P, (t + 1) * P)
+            nc.tensor.matmul_mx(
+                out=bank,
+                lhsT=lhs_codes[:, rows].bitcast(FP8X4),
+                lhsT_scale=lhs_bytes[:, rows],
+                rhs=rhs_codes.bitcast(FP8X4),
+                rhs_scale=rhs_bytes,
+                start=True,
+                stop=True,
+            )
+
+        s_first = [psum.tile([P, HALF], F32, name="s_first%d" % c, tag="bank%d" % c) for c in range(2)]
+        s_rest = {t: psum.tile([P, S], F32, name="s_rest%d" % t, tag="bank%d" % (t + 1)) for t in range(1, PACK)}
+        for c in range(2):
+            nc.vector.tensor_copy(
+                x_codes[:, halves[c]], x_word_table[:].indirect(offs_sb[:, entries[c]])
+            )
+            product(s_first[c][:], d_codes, d_bytes, x_codes[:, halves[c]], x_bytes[:, halves[c]], 0)
+        for t in range(1, PACK):
+            product(s_rest[t][:], d_codes, d_bytes, x_codes[:], x_bytes, t)
+        w_bytes = sb("w_bytes", [P, S], U8, tag="x_word_table")
+        nc.vector.tensor_copy(dealt(w_bytes[:]), deal(w_bytes_raw[:]))
+        settle_scale_rows(nc.sync, w_bytes)
+
+
+        s_row = [sb("s_row%d" % t, [P, S], F32) for t in range(PACK)]
+        gs_row = [sb("gs_row%d" % t, [P, S], F32) for t in range(PACK)]
+        gs_n2 = [sb("gs_n2_%d" % c, [P, PACK, HALF], F32) for c in range(2)]
+        s_n1 = sb("s_n1", [P, HALF], F32)
+        first = [sb("first%d" % c, [P, PACK, HALF], F32) for c in range(2)]
+        second = [sb("second%d" % c, [P, PACK, HALF], F32) for c in range(2)]
+        z_bf = [sb("z_bf%d" % c, [P, HALF, PACK], BF16) for c in range(2)]
+        z_codes = [sb("z_codes%d" % c, [P, HALF], U32) for c in range(2)]
+        z_bytes = [sb("z_bytes%d" % c, [P, HALF], U8) for c in range(2)]
+
+        def by_planes(ap):
+            return ap.rearrange("p t (c i) -> p c t i", i=4)
+
+        def woven(ap):
+            return ap.rearrange("p (c i) t -> p c t i", i=4)
+
+        def s_out(t, cols, bank):
+            nc.scalar.activation(s_row[t][:, cols], bank[:], ACT.Copy, scale=0.0625)
+            nc.scalar.activation(gs_row[t][:, cols], bank[:], ACT.Copy, scale=gain[:, t : t + 1])
+
+        def fetch_n2(t, c):
+            nc.scalar.activation(
+                gs_n2[c][:, t, :], gs_row[t][:].indirect(n2_sb[:, entries[c]]), ACT.Copy
+            )
+
+        def first_product(t, c):
+            nc.vector.tensor_tensor(
+                first[c][:, t, :], s_row[t][:].indirect(n1_sb[:, entries[c]]),
+                gs_row[t][:, halves[c]], ALU.mult,
+            )
+
+        def second_product(t, c):
+            nc.vector.tensor_tensor(
+                second[c][:, t, :], s_row[t][:].indirect(n3_sb[:, entries[c]]),
+                gs_n2[c][:, t, :], ALU.mult,
+            )
+
+        h_bank = {}
+        h_row = [sb("h_row%d" % t, [P, S], F32) for t in range(PACK)]
+        sq_row = [sb("sq_row%d" % t, [P, S], F32) for t in range(PACK)]
+        sq_copy = sb("sq_copy", [P, HALF], F32)
+
+        def z_sum(c):
+            nc.vector.tensor_tensor(
+                woven(z_bf[c][:]), by_planes(first[c][:]), by_planes(second[c][:]), ALU.add
+            )
+
+        def h_product(c):
+            nc.vector.quantize_mx(
+                out=z_codes[c][:].bitcast(FP8X4), scales=z_bytes[c][:],
+                in_=z_bf[c][:].rearrange("p j t -> p (j t)"),
+            )
+            for t in range(PACK):
+                h_bank[t, c] = psum.tile([P, HALF], F32, name="h_bank", tag="bank%d" % (PACK * c + t))
+                product(h_bank[t, c][:], w_codes, w_bytes, z_codes[c][:], z_bytes[c][:], t)
+
+        def sq_out(t, c):
+            nc.scalar.activation(sq_row[t][:, halves[c]], h_bank[t, c][:], ACT.Square)
+
+        def h_out(t, c):
+            nc.scalar.activation(h_row[t][:, halves[c]], h_bank[t, c][:], ACT.Copy)
+
+        def h_out_vector(t, c):
+            nc.vector.tensor_copy(h_row[t][:, halves[c]], h_bank[t, c][:])
+
+        for c in range(2):
+            s_out(0, halves[c], s_first[c])
+        for t in range(2):
+            if t > 0:
+                s_out(t, slice(0, S), s_rest[t])
+            for c in range(2):
+                first_product(t, c)
+                fetch_n2(t, c)
+            for c in range(2):
+                second_product(t, c)
+        s_out(2, slice(0, S), s_rest[2])
+        first_product(2, 0)
+        fetch_n2(2, 0)
+        second_product(2, 0)
+        s_out(3, slice(0, S), s_rest[3])
+        first_product(2, 1)
+        first_product(3, 0)
+        fetch_n2(3, 0)
+        second_product(3, 0)
+        fetch_n2(2, 1)
+        fetch_n2(3, 1)
+        w_codes = sb("w_codes", [P, S], U32, tag="x_codes")
+        nc.scalar.copy(dealt(w_codes[:]), deal(w_words_raw[:]))
+        nc.scalar.activation(s_n1[:], s_row[3][:].indirect(n1_sb[:, entries[1]]), ACT.Copy)
+        z_sum(0)
+        second_product(2, 1)
+        h_product(0)
+        nc.vector.tensor_tensor(first[1][:, 3, :], s_n1[:], gs_row[3][:, halves[1]], ALU.mult)
+        second_product(3, 1)
+        for t in range(PACK):
+            sq_out(t, 0)
+            h_out(t, 0)
+        nc.scalar.activation(sq_copy[:], h_bank[0, 0][:], ACT.Square)
+        z_sum(1)
+        h_product(1)
+
+
+        sq_n4 = [sb("sq_n4_%d" % c, [P, PACK, HALF], F32) for c in range(2)]
+        total = [sb("total%d" % c, [P, PACK, HALF], F32) for c in range(2)]
+        inv_root = [sb("inv_root%d" % c, [P, PACK, HALF], F32) for c in range(2)]
+        result = [sb("result%d" % c, [P, PACK, HALF], F32) for c in range(2)]
+        result_bf = [sb("result_bf%d" % c, [P, HALF, PACK], BF16) for c in range(2)]
+        out_codes = sb("out_codes", [P, S], U32)
+        out_bytes = sb("out_bytes", [P, S], U8)
+        out_rows = out_0.rearrange("(p t) j -> p t j", t=PACK)
+        out_words = words_view(out_1)
+        quarter = sb("quarter", [P, 1], F32)
+        nc.gpsimd.memset(quarter[:], 0.25)
+
+        def fetch_n4(t, c):
+            nc.scalar.activation(
+                sq_n4[c][:, t, :], sq_row[t][:].indirect(n4_sb[:, entries[c]]), ACT.Copy
+            )
+
+        def add_squares(t, c):
+            nc.vector.tensor_tensor(
+                total[c][:, t, :], sq_n4[c][:, t, :], sq_row[t][:, halves[c]], ALU.add
+            )
+
+        def root(t, c):
+            nc.scalar.activation(
+                inv_root[c][:, t, :], total[c][:, t, :], ACT.Abs_reciprocal_sqrt, bias=quarter[:]
+            )
+
+        def quotient(t, c):
+            nc.vector.tensor_tensor(
+                result[c][:, t, :], h_row[t][:].indirect(n5_sb[:, entries[c]]),
+                inv_root[c][:, t, :], ALU.mult,
+            )
+            nc.sync.dma_start(out_rows[:, t, halves[c]], result[c][:, t, :])
+
+        def weave(c):
+            nc.vector.tensor_copy(woven(result_bf[c][:]), by_planes(result[c][:]))
+
+        def planes(c):
+            nc.vector.quantize_mx(
+                out=out_codes[:, halves[c]].bitcast(FP8X4), scales=out_bytes[:, halves[c]],
+                in_=result_bf[c][:].rearrange("p j t -> p (j t)"),
+            )
+            nc.sync.dma_start(out_words[:, halves[c]], out_codes[:, halves[c]].bitcast(I32))
+
+        sq_out(0, 1)
+        h_out_vector(1, 1)
+        nc.vector.tensor_tensor(
+            total[0][:, 0, :], sq_row[0][:].indirect(n4_sb[:, entries[0]]), sq_copy[:], ALU.add
+        )
+        fetch_n4(0, 1)
+        h_out_vector(0, 1)
+        steps = [(0, 0), (0, 1), (1, 0), (1, 1), (2, 0), (3, 0), (2, 1), (3, 1)]
+        for k, (t, c) in enumerate(steps):
+            root(t, c)
+            if k + 1 < len(steps):
+                add_squares(*steps[k + 1])
+            if k + 2 < len(steps):
+                ahead, ahead_half = steps[k + 2]
+                if ahead_half == 0:
+                    sq_out(ahead, 1)
+                fetch_n4(ahead, ahead_half)
+                if ahead_half == 0 and ahead > 1:
+                    h_out(ahead, 1)
+            quotient(t, c)
+            if (t, c) == (3, 0):
+                weave(0)
+            if (t, c) == (2, 1):
+                planes(0)
+        part = HALF // 2
+        nc.vector.tensor_copy(woven(result_bf[1][:, :part, :]), by_planes(result[1][:, :, :part]))
+        nc.scalar.copy(woven(result_bf[1][:, part:, :]), by_planes(result[1][:, :, part:]))
+        planes(1)
+        for q in range(4):
+            queue = nc.scalar if q % 2 else nc.sync
+            queue.dma_start(
+                out_2[0, 4 * q : 4 * q + 4, :].bitcast(I32),
+                out_bytes[32 * q : 32 * q + 4, :].bitcast(I32),
+            )

@@ -89,7 +89,10 @@ def tile_picked_keydotrms_none_po_kernel(
         d_bytes = dx_bytes[:, :S]
         x_bytes = dx_bytes[:, S:]
         gain = sb("gain", [P, PACK], F32)
-
+        quarter = sb("quarter", [P, 1], F32)
+        nc.gpsimd.memset(quarter[:], 0.25)
+        warm_up = sb("warm_up", [P, 1], F32)
+        nc.scalar.activation(warm_up[:], quarter[:], ACT.Abs_reciprocal_sqrt)
         nc.scalar.activation(gain[:], gn_sb[:], ACT.Copy, scale=0.75 * 0.0625)
         nc.vector.tensor_copy(d_bytes_picked[:], d_byte_table[:].indirect(kidx_sb[:]))
         nc.vector.tensor_copy(x_bytes_picked[:], x_byte_table[:].indirect(offs_sb[:]))
@@ -239,8 +242,6 @@ def tile_picked_keydotrms_none_po_kernel(
         out_bytes = sb("out_bytes", [P, S], U8)
         out_rows = out_0.rearrange("(p t) j -> p t j", t=PACK)
         out_words = words_view(out_1)
-        quarter = sb("quarter", [P, 1], F32)
-        nc.gpsimd.memset(quarter[:], 0.25)
 
         def fetch_n4(t, c):
             nc.scalar.activation(

@@ -13,10 +13,12 @@ ACT = mybir.ActivationFunctionType
 ALU = mybir.AluOpType
 
 P = 128
-PACK = 4
+PLANES = 4
 TABLE = 2048
 S = 512
-HALF = 256
+HALF = S // 2
+LINE = 4
+VECTOR_WEAVES = 176
 FLOPS = 2 * 2 * 512 * 512 * 512
 
 
@@ -25,153 +27,156 @@ def tile_picked_keydotrms_none_po_kernel(
     offs, kidx, n1, n2, n3, n4, n5, out_0, out_1, out_2,
 ):
     nc = tc.nc
-    halves = [slice(c * HALF, (c + 1) * HALF) for c in range(2)]
-    entries = [slice(c * HALF // 16, (c + 1) * HALF // 16) for c in range(2)]
+    halves = [slice(0, HALF), slice(HALF, S)]
+    whole = slice(0, S)
 
     with ExitStack() as ctx:
         lists = ctx.enter_context(tc.tile_pool(name="lists", bufs=1))
         keep = ctx.enter_context(tc.tile_pool(name="keep", bufs=1))
         psum = ctx.enter_context(tc.psum_pool(name="psum", bufs=1))
 
-        def sb(name, shape, dtype, tag=None):
-            return keep.tile(shape, dtype, name=name, tag=tag or name, align_bytes=64)
+        def sbuf(name, shape, dtype, in_place_of=None):
+            return keep.tile(shape, dtype, name=name, tag=in_place_of or name, align_bytes=64)
 
         def load_list(name, src):
             tile = lists.tile([P, S // 16], U16, name=name)
             nc.sync.dma_start(tile[:], src)
             return tile
 
-        def words_view(src):
-            return src[0].rearrange("p n t -> p (n t)").bitcast(I32)
+        def as_words(packed):
+            return packed[0].rearrange("p n t -> p (n t)").bitcast(I32)
 
-        def load_scale_rows(tile, src):
-            rows = src[0].bitcast(I32)
-            nc.sync.dma_start(
-                tile[:].bitcast(I32), rows.unsqueeze(1).to_broadcast([16, 8, rows.shape[1]])
-            )
-
-        def deal(ap):
-            return ap.rearrange("p (m t) -> p t m", t=PACK)
-
-        def dealt(ap):
-            return ap.rearrange("p (t m) -> p t m", t=PACK)
+        def load_rows_by_run(tile, scales):
+            nc.sync.dma_start(tile[0:P:8, :].bitcast(I32), scales[0].bitcast(I32))
 
         def settle_scale_rows(queue, tile):
             for r in range(1, 4):
                 queue.dma_start(tile[r:P:32, :].bitcast(I32), tile[8 * r : P : 32, :].bitcast(I32))
 
-        d_byte_table = sb("d_byte_table", [P, TABLE], U8)
-        x_byte_table = sb("x_byte_table", [P, TABLE], U8)
-        d_word_table = sb("d_word_table", [P, TABLE], U32)
-        x_word_table = sb("x_word_table", [P, TABLE], U32)
-        w_bytes_raw = sb("w_bytes_raw", [P, S], U8)
-        w_words_raw = sb("w_words_raw", [P, S], U32)
-        gn_sb = sb("gn_sb", [P, PACK], F32)
+        def deal(copy, dst, src):
+            copy(
+                dst.rearrange("p (t m) -> p t m", t=PLANES), src.rearrange("p (m t) -> p t m", t=PLANES)
+            )
 
-        kidx_sb = load_list("kidx_sb", kidx)
-        load_scale_rows(d_byte_table, d_scales)
-        offs_sb = load_list("offs_sb", offs)
-        load_scale_rows(x_byte_table, x_scales)
-        nc.sync.dma_start(gn_sb[:], gn.rearrange("(p t) o -> p (t o)", t=PACK))
-        nc.sync.dma_start(d_word_table[:].bitcast(I32), words_view(d_words))
-        n1_sb = load_list("n1_sb", n1)
-        n2_sb = load_list("n2_sb", n2)
-        n3_sb = load_list("n3_sb", n3)
-        nc.sync.dma_start(x_word_table[:].bitcast(I32), words_view(x_words))
-        n4_sb = load_list("n4_sb", n4)
-        n5_sb = load_list("n5_sb", n5)
-        nc.sync.dma_start(w_words_raw[:].bitcast(I32), words_view(w1_words))
-        load_scale_rows(w_bytes_raw, w1_scales)
+        def looked_up(window, offsets, cols):
+            return window[:].indirect(offsets[:, cols.start // 16 : cols.stop // 16])
 
-        d_bytes_picked = sb("d_bytes_picked", [P, S], U8)
-        x_bytes_picked = sb("x_bytes_picked", [P, S], U8)
-        dx_bytes = sb("dx_bytes", [P, 2 * S], U8)
-        d_bytes = dx_bytes[:, :S]
-        x_bytes = dx_bytes[:, S:]
-        gain = sb("gain", [P, PACK], F32)
-        quarter = sb("quarter", [P, 1], F32)
-        nc.gpsimd.memset(quarter[:], 0.25)
-        warm_up = sb("warm_up", [P, 1], F32)
-        nc.scalar.activation(warm_up[:], quarter[:], ACT.Abs_reciprocal_sqrt)
-        nc.scalar.activation(gain[:], gn_sb[:], ACT.Copy, scale=0.75 * 0.0625)
-        nc.vector.tensor_copy(d_bytes_picked[:], d_byte_table[:].indirect(kidx_sb[:]))
-        nc.vector.tensor_copy(x_bytes_picked[:], x_byte_table[:].indirect(offs_sb[:]))
-        nc.vector.tensor_copy(dealt(d_bytes), deal(d_bytes_picked[:]))
-        nc.vector.tensor_copy(x_bytes.bitcast(I32), x_bytes_picked[:].bitcast(I32))
-        settle_scale_rows(nc.scalar, dx_bytes)
-        d_words_picked = sb("d_words_picked", [P, S], U32)
-        d_codes = sb("d_codes", [P, S], U32)
-        nc.vector.tensor_copy(d_words_picked[:], d_word_table[:].indirect(kidx_sb[:]))
-        nc.vector.tensor_copy(dealt(d_codes[:]), deal(d_words_picked[:]))
-        x_codes = sb("x_codes", [P, S], U32)
+        def fetch(dst, window, offsets, cols):
+            nc.scalar.activation(dst, looked_up(window, offsets, cols), ACT.Copy)
 
-        def product(bank, lhs_codes, lhs_bytes, rhs_codes, rhs_bytes, t):
-            rows = slice(t * P, (t + 1) * P)
+        def product(bank, lhs_codes, lhs_bytes, t, rhs_codes, rhs_bytes):
+            plane = slice(t * P, (t + 1) * P)
             nc.tensor.matmul_mx(
-                out=bank,
-                lhsT=lhs_codes[:, rows].bitcast(FP8X4),
-                lhsT_scale=lhs_bytes[:, rows],
+                out=bank[:],
+                lhsT=lhs_codes[:, plane].bitcast(FP8X4),
+                lhsT_scale=lhs_bytes[:, plane],
                 rhs=rhs_codes.bitcast(FP8X4),
                 rhs_scale=rhs_bytes,
                 start=True,
                 stop=True,
             )
 
-        s_first = [psum.tile([P, HALF], F32, name="s_first%d" % c, tag="bank%d" % c) for c in range(2)]
-        s_rest = {t: psum.tile([P, S], F32, name="s_rest%d" % t, tag="bank%d" % (t + 1)) for t in range(1, PACK)}
-        for c in range(2):
-            nc.vector.tensor_copy(
-                x_codes[:, halves[c]], x_word_table[:].indirect(offs_sb[:, entries[c]])
-            )
-            product(s_first[c][:], d_codes, d_bytes, x_codes[:, halves[c]], x_bytes[:, halves[c]], 0)
-        for t in range(1, PACK):
-            product(s_rest[t][:], d_codes, d_bytes, x_codes[:], x_bytes, t)
-        w_bytes = sb("w_bytes", [P, S], U8, tag="x_word_table")
-        nc.vector.tensor_copy(dealt(w_bytes[:]), deal(w_bytes_raw[:]))
-        settle_scale_rows(nc.sync, w_bytes)
-
-
-        s_row = [sb("s_row%d" % t, [P, S], F32) for t in range(PACK)]
-        gs_row = [sb("gs_row%d" % t, [P, S], F32) for t in range(PACK)]
-        gs_n2 = [sb("gs_n2_%d" % c, [P, PACK, HALF], F32) for c in range(2)]
-        s_n1 = sb("s_n1", [P, HALF], F32)
-        first = [sb("first%d" % c, [P, PACK, HALF], F32) for c in range(2)]
-        second = [sb("second%d" % c, [P, PACK, HALF], F32) for c in range(2)]
-        z_bf = [sb("z_bf%d" % c, [P, HALF, PACK], BF16) for c in range(2)]
-        z_codes = [sb("z_codes%d" % c, [P, HALF], U32) for c in range(2)]
-        z_bytes = [sb("z_bytes%d" % c, [P, HALF], U8) for c in range(2)]
-
         def by_planes(ap):
-            return ap.rearrange("p t (c i) -> p c t i", i=4)
+            return ap.rearrange("p t (c i) -> p c t i", i=LINE)
 
         def woven(ap):
-            return ap.rearrange("p (c i) t -> p c t i", i=4)
+            return ap.rearrange("p (c i) t -> p c t i", i=LINE)
+
+        d_byte_table = sbuf("d_byte_table", [P, TABLE], U8)
+        x_byte_table = sbuf("x_byte_table", [P, TABLE], U8)
+        d_word_table = sbuf("d_word_table", [P, TABLE], U32)
+        x_word_table = sbuf("x_word_table", [P, TABLE], U32)
+        w_words_loaded = sbuf("w_words_loaded", [P, S], U32)
+        gn_sb = sbuf("gn_sb", [P, PLANES], F32)
+        quarter = sbuf("quarter", [P, 1], F32)
+
+        nc.vector.memset(d_byte_table[:].bitcast(I32), 0)
+        nc.vector.memset(x_byte_table[:].bitcast(I32), 0)
+        nc.gpsimd.memset(quarter[:], 0.25)
+
+        load_rows_by_run(d_byte_table, d_scales)
+        load_rows_by_run(x_byte_table, x_scales)
+        kidx_sb = load_list("kidx_sb", kidx)
+        offs_sb = load_list("offs_sb", offs)
+        n1_sb = load_list("n1_sb", n1)
+        n2_sb = load_list("n2_sb", n2)
+        n3_sb = load_list("n3_sb", n3)
+        nc.sync.dma_start(d_word_table[:].bitcast(I32), as_words(d_words))
+        nc.sync.dma_start(x_word_table[:].bitcast(I32), as_words(x_words))
+        nc.sync.dma_start(w_words_loaded[:].bitcast(I32), as_words(w1_words))
+        n4_sb = load_list("n4_sb", n4)
+        n5_sb = load_list("n5_sb", n5)
+        nc.gpsimd.dma_start(gn_sb[:], gn.rearrange("(p t) o -> p (t o)", t=PLANES))
+
+        warm_up = sbuf("warm_up", [P, 1], F32)
+        nc.scalar.activation(warm_up[:], quarter[:], ACT.Abs_reciprocal_sqrt)
+
+        s_row = [sbuf("s_row%d" % t, [P, S], F32) for t in range(PLANES)]
+        gs_row = [sbuf("gs_row%d" % t, [P, S], F32) for t in range(PLANES)]
+
+        gain = sbuf("gain", [P, PLANES], F32)
+        nc.gpsimd.tensor_scalar(gain[:], gn_sb[:], 0.75 * 0.0625, 0.0, ALU.mult, ALU.add)
+
+        bytes_picked = sbuf("bytes_picked", [P, 2 * S], U8)
+        dx_bytes = sbuf("dx_bytes", [P, 2 * S], U8)
+        d_bytes, x_bytes = dx_bytes[:, :S], dx_bytes[:, S:]
+        nc.vector.tensor_copy(bytes_picked[:, :S], looked_up(d_byte_table, kidx_sb, whole))
+        nc.vector.tensor_copy(bytes_picked[:, S:], looked_up(x_byte_table, offs_sb, whole))
+        deal(nc.vector.tensor_copy, d_bytes, bytes_picked[:, :S])
+        nc.vector.tensor_copy(x_bytes.bitcast(I32), bytes_picked[:, S:].bitcast(I32))
+        settle_scale_rows(nc.scalar, dx_bytes)
+        w_bytes_loaded = sbuf("w_bytes_loaded", [P, S], U8, in_place_of="x_byte_table")
+        nc.gpsimd.memset(w_bytes_loaded[:].bitcast(I32), 0)
+        load_rows_by_run(w_bytes_loaded, w1_scales)
+
+        d_words_picked = sbuf("d_words_picked", [P, S], U32, in_place_of="bytes_picked")
+        d_codes = sbuf("d_codes", [P, S], U32)
+        nc.vector.tensor_copy(d_words_picked[:], looked_up(d_word_table, kidx_sb, whole))
+        deal(nc.vector.tensor_copy, d_codes[:], d_words_picked[:])
+        w_codes = sbuf("w_codes", [P, S], U32)
+        deal(nc.scalar.copy, w_codes[:], w_words_loaded[:])
+
+        x_codes = sbuf("x_codes", [P, S], U32)
+        s_bank = {}
+        for c, cols in enumerate(halves):
+            nc.vector.tensor_copy(x_codes[:, cols], looked_up(x_word_table, offs_sb, cols))
+            s_bank[0, c] = psum.tile([P, HALF], F32, name="s_half", tag="bank%d" % c)
+            product(s_bank[0, c], d_codes, d_bytes, 0, x_codes[:, cols], x_bytes[:, cols])
+        for t in range(1, PLANES):
+            s_bank[t] = psum.tile([P, S], F32, name="s_plane", tag="bank%d" % (t + 1))
+            product(s_bank[t], d_codes, d_bytes, t, x_codes[:], x_bytes)
+        w_bytes = sbuf("w_bytes", [P, S], U8, in_place_of="x_word_table")
+        deal(nc.vector.tensor_copy, w_bytes[:], w_bytes_loaded[:])
+        settle_scale_rows(nc.sync, w_bytes)
+
+        gs_n2 = [sbuf("gs_n2_%d" % c, [P, PLANES, HALF], F32) for c in range(2)]
+        first = [sbuf("first%d" % c, [P, PLANES, HALF], F32) for c in range(2)]
+        second = [sbuf("second%d" % c, [P, PLANES, HALF], F32) for c in range(2)]
+        z_bf = [sbuf("z_bf%d" % c, [P, HALF, PLANES], BF16) for c in range(2)]
+        z_codes = [sbuf("z_codes%d" % c, [P, HALF], U32) for c in range(2)]
+        z_bytes = [sbuf("z_bytes%d" % c, [P, HALF], U8) for c in range(2)]
+        h_row = [sbuf("h_row%d" % t, [P, S], F32) for t in range(PLANES)]
+        sq_row = [sbuf("sq_row%d" % t, [P, S], F32) for t in range(PLANES)]
+        h_bank = {}
 
         def s_out(t, cols, bank):
             nc.scalar.activation(s_row[t][:, cols], bank[:], ACT.Copy, scale=0.0625)
+
+        def gs_out(t, cols, bank):
             nc.scalar.activation(gs_row[t][:, cols], bank[:], ACT.Copy, scale=gain[:, t : t + 1])
 
-        def fetch_n2(t, c):
-            nc.scalar.activation(
-                gs_n2[c][:, t, :], gs_row[t][:].indirect(n2_sb[:, entries[c]]), ACT.Copy
-            )
+        def fetch_gs(t, c):
+            fetch(gs_n2[c][:, t, :], gs_row[t], n2_sb, halves[c])
 
-        def first_product(t, c):
+        def first_term(t, c):
             nc.vector.tensor_tensor(
-                first[c][:, t, :], s_row[t][:].indirect(n1_sb[:, entries[c]]),
-                gs_row[t][:, halves[c]], ALU.mult,
+                first[c][:, t, :], looked_up(s_row[t], n1_sb, halves[c]), gs_row[t][:, halves[c]], ALU.mult
             )
 
-        def second_product(t, c):
+        def second_term(t, c):
             nc.vector.tensor_tensor(
-                second[c][:, t, :], s_row[t][:].indirect(n3_sb[:, entries[c]]),
-                gs_n2[c][:, t, :], ALU.mult,
+                second[c][:, t, :], looked_up(s_row[t], n3_sb, halves[c]), gs_n2[c][:, t, :], ALU.mult
             )
-
-        h_bank = {}
-        h_row = [sb("h_row%d" % t, [P, S], F32) for t in range(PACK)]
-        sq_row = [sb("sq_row%d" % t, [P, S], F32) for t in range(PACK)]
-        sq_copy = sb("sq_copy", [P, HALF], F32)
 
         def z_sum(c):
             nc.vector.tensor_tensor(
@@ -183,9 +188,9 @@ def tile_picked_keydotrms_none_po_kernel(
                 out=z_codes[c][:].bitcast(FP8X4), scales=z_bytes[c][:],
                 in_=z_bf[c][:].rearrange("p j t -> p (j t)"),
             )
-            for t in range(PACK):
-                h_bank[t, c] = psum.tile([P, HALF], F32, name="h_bank", tag="bank%d" % (PACK * c + t))
-                product(h_bank[t, c][:], w_codes, w_bytes, z_codes[c][:], z_bytes[c][:], t)
+            for t in range(PLANES):
+                h_bank[t, c] = psum.tile([P, HALF], F32, name="h_half", tag="bank%d" % (PLANES * c + t))
+                product(h_bank[t, c], w_codes, w_bytes, t, z_codes[c][:], z_bytes[c][:])
 
         def sq_out(t, c):
             nc.scalar.activation(sq_row[t][:, halves[c]], h_bank[t, c][:], ACT.Square)
@@ -193,65 +198,69 @@ def tile_picked_keydotrms_none_po_kernel(
         def h_out(t, c):
             nc.scalar.activation(h_row[t][:, halves[c]], h_bank[t, c][:], ACT.Copy)
 
-        def h_out_vector(t, c):
-            nc.vector.tensor_copy(h_row[t][:, halves[c]], h_bank[t, c][:])
-
+        for c, cols in enumerate(halves):
+            s_out(0, cols, s_bank[0, c])
+            gs_out(0, cols, s_bank[0, c])
         for c in range(2):
-            s_out(0, halves[c], s_first[c])
-        for t in range(2):
-            if t > 0:
-                s_out(t, slice(0, S), s_rest[t])
-            for c in range(2):
-                first_product(t, c)
-                fetch_n2(t, c)
-            for c in range(2):
-                second_product(t, c)
-        s_out(2, slice(0, S), s_rest[2])
-        first_product(2, 0)
-        fetch_n2(2, 0)
-        second_product(2, 0)
-        s_out(3, slice(0, S), s_rest[3])
-        first_product(2, 1)
-        first_product(3, 0)
-        fetch_n2(3, 0)
-        second_product(3, 0)
-        fetch_n2(2, 1)
-        fetch_n2(3, 1)
-        w_codes = sb("w_codes", [P, S], U32, tag="x_codes")
-        nc.scalar.copy(dealt(w_codes[:]), deal(w_words_raw[:]))
-        nc.scalar.activation(s_n1[:], s_row[3][:].indirect(n1_sb[:, entries[1]]), ACT.Copy)
+            first_term(0, c)
+        last = PLANES - 1
+        for t in range(1, PLANES):
+            s_out(t, whole, s_bank[t])
+            fetch_gs(t - 1, 0)
+            second_term(t - 1, 0)
+            gs_out(t, whole, s_bank[t])
+            first_term(t, 0)
+            fetch_gs(t - 1, 1)
+            if t < last:
+                second_term(t - 1, 1)
+                first_term(t, 1)
+        fetch_gs(last, 0)
+        second_term(last, 0)
+        fetch_gs(last, 1)
+
+        late = halves[1]
+        s_n1 = sbuf("s_n1", [P, HALF], F32)
+        s_n3 = {t: sbuf("s_n3_%d" % t, [P, HALF], F32) for t in (last - 1, last)}
+        fetch(s_n3[last - 1][:], s_row[last - 1], n3_sb, late)
+        fetch(s_n1[:], s_row[last], n1_sb, late)
+        fetch(s_n3[last][:], s_row[last], n3_sb, late)
+
+        def late_second_term(t):
+            nc.vector.tensor_tensor(second[1][:, t, :], s_n3[t][:], gs_n2[1][:, t, :], ALU.mult)
+
         z_sum(0)
-        second_product(2, 1)
+        late_second_term(last - 1)
         h_product(0)
-        nc.vector.tensor_tensor(first[1][:, 3, :], s_n1[:], gs_row[3][:, halves[1]], ALU.mult)
-        second_product(3, 1)
-        for t in range(PACK):
+        nc.vector.tensor_tensor(first[1][:, last, :], s_n1[:], gs_row[last][:, late], ALU.mult)
+        late_second_term(last)
+
+        sq_aside = sbuf("sq_aside", [P, PLANES, HALF], F32)
+        for t in range(PLANES):
             sq_out(t, 0)
-            h_out(t, 0)
-        nc.scalar.activation(sq_copy[:], h_bank[0, 0][:], ACT.Square)
+            nc.sync.dma_start(sq_aside[:, t, :], sq_row[t][:, halves[0]])
         z_sum(1)
         h_product(1)
+        for t in range(2):
+            h_out(t, 0)
+        for t in range(2, PLANES):
+            nc.vector.tensor_copy(h_row[t][:, halves[0]], h_bank[t, 0][:])
 
-
-        sq_n4 = [sb("sq_n4_%d" % c, [P, PACK, HALF], F32) for c in range(2)]
-        total = [sb("total%d" % c, [P, PACK, HALF], F32) for c in range(2)]
-        inv_root = [sb("inv_root%d" % c, [P, PACK, HALF], F32) for c in range(2)]
-        result = [sb("result%d" % c, [P, PACK, HALF], F32) for c in range(2)]
-        result_bf = [sb("result_bf%d" % c, [P, HALF, PACK], BF16) for c in range(2)]
-        out_codes = sb("out_codes", [P, S], U32)
-        out_bytes = sb("out_bytes", [P, S], U8)
-        out_rows = out_0.rearrange("(p t) j -> p t j", t=PACK)
-        out_words = words_view(out_1)
-
-        def fetch_n4(t, c):
-            nc.scalar.activation(
-                sq_n4[c][:, t, :], sq_row[t][:].indirect(n4_sb[:, entries[c]]), ACT.Copy
-            )
+        sq_n4 = sbuf("sq_n4", [P, PLANES, HALF], F32)
+        h_n5 = {t: sbuf("h_n5_%d" % t, [P, HALF], F32) for t in (last - 1, last)}
+        total = [sbuf("total%d" % c, [P, PLANES, HALF], F32) for c in range(2)]
+        inv_root = [sbuf("inv_root%d" % c, [P, PLANES, HALF], F32) for c in range(2)]
+        result = [sbuf("result%d" % c, [P, PLANES, HALF], F32) for c in range(2)]
+        result_bf = [sbuf("result_bf%d" % c, [P, HALF, PLANES], BF16) for c in range(2)]
+        out_codes = sbuf("out_codes", [P, S], U32)
+        out_bytes = sbuf("out_bytes", [P, S], U8)
+        out_rows = out_0.rearrange("(p t) j -> p t j", t=PLANES)
 
         def add_squares(t, c):
-            nc.vector.tensor_tensor(
-                total[c][:, t, :], sq_n4[c][:, t, :], sq_row[t][:, halves[c]], ALU.add
-            )
+            if c == 0:
+                other, own = looked_up(sq_row[t], n4_sb, halves[0]), sq_aside[:, t, :]
+            else:
+                other, own = sq_n4[:, t, :], sq_row[t][:, late]
+            nc.vector.tensor_tensor(total[c][:, t, :], other, own, ALU.add)
 
         def root(t, c):
             nc.scalar.activation(
@@ -259,50 +268,49 @@ def tile_picked_keydotrms_none_po_kernel(
             )
 
         def quotient(t, c):
-            nc.vector.tensor_tensor(
-                result[c][:, t, :], h_row[t][:].indirect(n5_sb[:, entries[c]]),
-                inv_root[c][:, t, :], ALU.mult,
-            )
+            if c == 1 and t in h_n5:
+                numerator = h_n5[t][:]
+            else:
+                numerator = looked_up(h_row[t], n5_sb, halves[c])
+            nc.vector.tensor_tensor(result[c][:, t, :], numerator, inv_root[c][:, t, :], ALU.mult)
             nc.sync.dma_start(out_rows[:, t, halves[c]], result[c][:, t, :])
 
-        def weave(c):
-            nc.vector.tensor_copy(woven(result_bf[c][:]), by_planes(result[c][:]))
-
-        def planes(c):
+        def quantise_result(c):
+            cols = halves[c]
             nc.vector.quantize_mx(
-                out=out_codes[:, halves[c]].bitcast(FP8X4), scales=out_bytes[:, halves[c]],
+                out=out_codes[:, cols].bitcast(FP8X4), scales=out_bytes[:, cols],
                 in_=result_bf[c][:].rearrange("p j t -> p (j t)"),
             )
-            nc.sync.dma_start(out_words[:, halves[c]], out_codes[:, halves[c]].bitcast(I32))
+            nc.sync.dma_start(as_words(out_1)[:, cols], out_codes[:, cols].bitcast(I32))
 
+        steps = [(t, c) for c in range(2) for t in range(PLANES)]
         sq_out(0, 1)
-        h_out_vector(1, 1)
-        nc.vector.tensor_tensor(
-            total[0][:, 0, :], sq_row[0][:].indirect(n4_sb[:, entries[0]]), sq_copy[:], ALU.add
-        )
-        fetch_n4(0, 1)
-        h_out_vector(0, 1)
-        steps = [(0, 0), (0, 1), (1, 0), (1, 1), (2, 0), (3, 0), (2, 1), (3, 1)]
-        for k, (t, c) in enumerate(steps):
+        add_squares(0, 0)
+        sq_out(1, 1)
+        h_out(0, 1)
+        for k, (t, c) in enumerate(steps[:-1]):
             root(t, c)
-            if k + 1 < len(steps):
-                add_squares(*steps[k + 1])
-            if k + 2 < len(steps):
-                ahead, ahead_half = steps[k + 2]
-                if ahead_half == 0:
-                    sq_out(ahead, 1)
-                fetch_n4(ahead, ahead_half)
-                if ahead_half == 0 and ahead > 1:
-                    h_out(ahead, 1)
+            add_squares(*steps[k + 1])
+            if k + 1 < PLANES:
+                h_out(k + 1, 1)
+            if k + 2 < PLANES:
+                sq_out(k + 2, 1)
+            elif k + 2 < len(steps):
+                ahead = k + 2 - PLANES
+                fetch(sq_n4[:, ahead, :], sq_row[ahead], n4_sb, late)
+            if c == 1 and t + 1 in h_n5:
+                fetch(h_n5[t + 1][:], h_row[t + 1], n5_sb, late)
             quotient(t, c)
-            if (t, c) == (3, 0):
-                weave(0)
-            if (t, c) == (2, 1):
-                planes(0)
-        part = HALF // 2
-        nc.vector.tensor_copy(woven(result_bf[1][:, :part, :]), by_planes(result[1][:, :, :part]))
-        nc.scalar.copy(woven(result_bf[1][:, part:, :]), by_planes(result[1][:, :, part:]))
-        planes(1)
+            if (t, c) == (last, 0):
+                nc.vector.tensor_copy(woven(result_bf[0][:]), by_planes(result[0][:]))
+            if (t, c) == (0, 1):
+                quantise_result(0)
+        root(*steps[-1])
+        quotient(*steps[-1])
+        cut = VECTOR_WEAVES
+        nc.vector.tensor_copy(woven(result_bf[1][:, :cut, :]), by_planes(result[1][:, :, :cut]))
+        nc.scalar.copy(woven(result_bf[1][:, cut:, :]), by_planes(result[1][:, :, cut:]))
+        quantise_result(1)
         for q in range(4):
             queue = nc.scalar if q % 2 else nc.sync
             queue.dma_start(

from contextlib import ExitStack

import concourse.mybir as mybir

F32 = mybir.dt.float32
BF16 = mybir.dt.bfloat16
I32 = mybir.dt.int32
U32 = mybir.dt.uint32
U16 = mybir.dt.uint16
U8 = mybir.dt.uint8
FP8X4 = mybir.dt.float8_e4m3fn_x4
ACT = mybir.ActivationFunctionType
ALU = mybir.AluOpType

P = 128
PLANES = 4
TABLE = 2048
S = 512
HALF = S // 2
LINE = 4
VECTOR_WEAVES = 176
FLOPS = 2 * 2 * 512 * 512 * 512


def tile_picked_keydotrms_none_po_kernel(
    tc, x_words, x_scales, d_words, d_scales, gn, w1_words, w1_scales,
    offs, kidx, n1, n2, n3, n4, n5, out_0, out_1, out_2,
):
    nc = tc.nc
    halves = [slice(0, HALF), slice(HALF, S)]
    whole = slice(0, S)

    with ExitStack() as ctx:
        lists = ctx.enter_context(tc.tile_pool(name="lists", bufs=1))
        keep = ctx.enter_context(tc.tile_pool(name="keep", bufs=1))
        psum = ctx.enter_context(tc.psum_pool(name="psum", bufs=1))

        def sbuf(name, shape, dtype, in_place_of=None):
            return keep.tile(shape, dtype, name=name, tag=in_place_of or name, align_bytes=64)

        def load_list(name, src):
            tile = lists.tile([P, S // 16], U16, name=name)
            nc.sync.dma_start(tile[:], src)
            return tile

        def as_words(packed):
            return packed[0].rearrange("p n t -> p (n t)").bitcast(I32)

        def load_rows_by_run(tile, scales):
            nc.sync.dma_start(tile[0:P:8, :].bitcast(I32), scales[0].bitcast(I32))

        def settle_scale_rows(queue, tile):
            for r in range(1, 4):
                queue.dma_start(tile[r:P:32, :].bitcast(I32), tile[8 * r : P : 32, :].bitcast(I32))

        def deal(copy, dst, src):
            copy(
                dst.rearrange("p (t m) -> p t m", t=PLANES), src.rearrange("p (m t) -> p t m", t=PLANES)
            )

        def looked_up(window, offsets, cols):
            return window[:].indirect(offsets[:, cols.start // 16 : cols.stop // 16])

        def fetch(dst, window, offsets, cols):
            nc.scalar.activation(dst, looked_up(window, offsets, cols), ACT.Copy)

        def product(bank, lhs_codes, lhs_bytes, t, rhs_codes, rhs_bytes):
            plane = slice(t * P, (t + 1) * P)
            nc.tensor.matmul_mx(
                out=bank[:],
                lhsT=lhs_codes[:, plane].bitcast(FP8X4),
                lhsT_scale=lhs_bytes[:, plane],
                rhs=rhs_codes.bitcast(FP8X4),
                rhs_scale=rhs_bytes,
                start=True,
                stop=True,
            )

        def by_planes(ap):
            return ap.rearrange("p t (c i) -> p c t i", i=LINE)

        def woven(ap):
            return ap.rearrange("p (c i) t -> p c t i", i=LINE)

        d_byte_table = sbuf("d_byte_table", [P, TABLE], U8)
        x_byte_table = sbuf("x_byte_table", [P, TABLE], U8)
        d_word_table = sbuf("d_word_table", [P, TABLE], U32)
        x_word_table = sbuf("x_word_table", [P, TABLE], U32)
        w_words_loaded = sbuf("w_words_loaded", [P, S], U32)
        gn_sb = sbuf("gn_sb", [P, PLANES], F32)
        quarter = sbuf("quarter", [P, 1], F32)

        nc.vector.memset(d_byte_table[:].bitcast(I32), 0)
        nc.vector.memset(x_byte_table[:].bitcast(I32), 0)
        nc.gpsimd.memset(quarter[:], 0.25)

        load_rows_by_run(d_byte_table, d_scales)
        load_rows_by_run(x_byte_table, x_scales)
        kidx_sb = load_list("kidx_sb", kidx)
        offs_sb = load_list("offs_sb", offs)
        n1_sb = load_list("n1_sb", n1)
        n2_sb = load_list("n2_sb", n2)
        n3_sb = load_list("n3_sb", n3)
        nc.sync.dma_start(d_word_table[:].bitcast(I32), as_words(d_words))
        nc.sync.dma_start(x_word_table[:].bitcast(I32), as_words(x_words))
        nc.sync.dma_start(w_words_loaded[:].bitcast(I32), as_words(w1_words))
        n4_sb = load_list("n4_sb", n4)
        n5_sb = load_list("n5_sb", n5)
        nc.gpsimd.dma_start(gn_sb[:], gn.rearrange("(p t) o -> p (t o)", t=PLANES))

        warm_up = sbuf("warm_up", [P, 1], F32)
        nc.scalar.activation(warm_up[:], quarter[:], ACT.Abs_reciprocal_sqrt)

        s_row = [sbuf("s_row%d" % t, [P, S], F32) for t in range(PLANES)]
        gs_row = [sbuf("gs_row%d" % t, [P, S], F32) for t in range(PLANES)]

        gain = sbuf("gain", [P, PLANES], F32)
        nc.gpsimd.tensor_scalar(gain[:], gn_sb[:], 0.75 * 0.0625, 0.0, ALU.mult, ALU.add)

        bytes_picked = sbuf("bytes_picked", [P, 2 * S], U8)
        dx_bytes = sbuf("dx_bytes", [P, 2 * S], U8)
        d_bytes, x_bytes = dx_bytes[:, :S], dx_bytes[:, S:]
        nc.vector.tensor_copy(bytes_picked[:, :S], looked_up(d_byte_table, kidx_sb, whole))
        nc.vector.tensor_copy(bytes_picked[:, S:], looked_up(x_byte_table, offs_sb, whole))
        deal(nc.vector.tensor_copy, d_bytes, bytes_picked[:, :S])
        nc.vector.tensor_copy(x_bytes.bitcast(I32), bytes_picked[:, S:].bitcast(I32))
        settle_scale_rows(nc.scalar, dx_bytes)
        w_bytes_loaded = sbuf("w_bytes_loaded", [P, S], U8, in_place_of="x_byte_table")
        nc.gpsimd.memset(w_bytes_loaded[:].bitcast(I32), 0)
        load_rows_by_run(w_bytes_loaded, w1_scales)

        d_words_picked = sbuf("d_words_picked", [P, S], U32, in_place_of="bytes_picked")
        d_codes = sbuf("d_codes", [P, S], U32)
        nc.vector.tensor_copy(d_words_picked[:], looked_up(d_word_table, kidx_sb, whole))
        deal(nc.vector.tensor_copy, d_codes[:], d_words_picked[:])
        w_codes = sbuf("w_codes", [P, S], U32)
        deal(nc.scalar.copy, w_codes[:], w_words_loaded[:])

        x_codes = sbuf("x_codes", [P, S], U32)
        s_bank = {}
        for c, cols in enumerate(halves):
            nc.vector.tensor_copy(x_codes[:, cols], looked_up(x_word_table, offs_sb, cols))
            s_bank[0, c] = psum.tile([P, HALF], F32, name="s_half", tag="bank%d" % c)
            product(s_bank[0, c], d_codes, d_bytes, 0, x_codes[:, cols], x_bytes[:, cols])
        for t in range(1, PLANES):
            s_bank[t] = psum.tile([P, S], F32, name="s_plane", tag="bank%d" % (t + 1))
            product(s_bank[t], d_codes, d_bytes, t, x_codes[:], x_bytes)
        w_bytes = sbuf("w_bytes", [P, S], U8, in_place_of="x_word_table")
        deal(nc.vector.tensor_copy, w_bytes[:], w_bytes_loaded[:])
        settle_scale_rows(nc.sync, w_bytes)

        gs_n2 = [sbuf("gs_n2_%d" % c, [P, PLANES, HALF], F32) for c in range(2)]
        first = [sbuf("first%d" % c, [P, PLANES, HALF], F32) for c in range(2)]
        second = [sbuf("second%d" % c, [P, PLANES, HALF], F32) for c in range(2)]
        z_bf = [sbuf("z_bf%d" % c, [P, HALF, PLANES], BF16) for c in range(2)]
        z_codes = [sbuf("z_codes%d" % c, [P, HALF], U32) for c in range(2)]
        z_bytes = [sbuf("z_bytes%d" % c, [P, HALF], U8) for c in range(2)]
        h_row = [sbuf("h_row%d" % t, [P, S], F32) for t in range(PLANES)]
        sq_row = [sbuf("sq_row%d" % t, [P, S], F32) for t in range(PLANES)]
        h_bank = {}

        def s_out(t, cols, bank):
            nc.scalar.activation(s_row[t][:, cols], bank[:], ACT.Copy, scale=0.0625)

        def gs_out(t, cols, bank):
            nc.scalar.activation(gs_row[t][:, cols], bank[:], ACT.Copy, scale=gain[:, t : t + 1])

        def fetch_gs(t, c):
            fetch(gs_n2[c][:, t, :], gs_row[t], n2_sb, halves[c])

        def first_term(t, c):
            nc.vector.tensor_tensor(
                first[c][:, t, :], looked_up(s_row[t], n1_sb, halves[c]), gs_row[t][:, halves[c]], ALU.mult
            )

        def second_term(t, c):
            nc.vector.tensor_tensor(
                second[c][:, t, :], looked_up(s_row[t], n3_sb, halves[c]), gs_n2[c][:, t, :], ALU.mult
            )

        def z_sum(c):
            nc.vector.tensor_tensor(
                woven(z_bf[c][:]), by_planes(first[c][:]), by_planes(second[c][:]), ALU.add
            )

        def h_product(c):
            nc.vector.quantize_mx(
                out=z_codes[c][:].bitcast(FP8X4), scales=z_bytes[c][:],
                in_=z_bf[c][:].rearrange("p j t -> p (j t)"),
            )
            for t in range(PLANES):
                h_bank[t, c] = psum.tile([P, HALF], F32, name="h_half", tag="bank%d" % (PLANES * c + t))
                product(h_bank[t, c], w_codes, w_bytes, t, z_codes[c][:], z_bytes[c][:])

        def sq_out(t, c):
            nc.scalar.activation(sq_row[t][:, halves[c]], h_bank[t, c][:], ACT.Square)

        def h_out(t, c):
            nc.scalar.activation(h_row[t][:, halves[c]], h_bank[t, c][:], ACT.Copy)

        for c, cols in enumerate(halves):
            s_out(0, cols, s_bank[0, c])
            gs_out(0, cols, s_bank[0, c])
        for c in range(2):
            first_term(0, c)
        last = PLANES - 1
        for t in range(1, PLANES):
            s_out(t, whole, s_bank[t])
            fetch_gs(t - 1, 0)
            second_term(t - 1, 0)
            gs_out(t, whole, s_bank[t])
            first_term(t, 0)
            fetch_gs(t - 1, 1)
            if t < last:
                second_term(t - 1, 1)
                first_term(t, 1)
        fetch_gs(last, 0)
        second_term(last, 0)
        fetch_gs(last, 1)

        late = halves[1]
        s_n1 = sbuf("s_n1", [P, HALF], F32)
        s_n3 = {t: sbuf("s_n3_%d" % t, [P, HALF], F32) for t in (last - 1, last)}
        fetch(s_n3[last - 1][:], s_row[last - 1], n3_sb, late)
        fetch(s_n1[:], s_row[last], n1_sb, late)
        fetch(s_n3[last][:], s_row[last], n3_sb, late)

        def late_second_term(t):
            nc.vector.tensor_tensor(second[1][:, t, :], s_n3[t][:], gs_n2[1][:, t, :], ALU.mult)

        z_sum(0)
        late_second_term(last - 1)
        h_product(0)
        nc.vector.tensor_tensor(first[1][:, last, :], s_n1[:], gs_row[last][:, late], ALU.mult)
        late_second_term(last)

        sq_aside = sbuf("sq_aside", [P, PLANES, HALF], F32)
        for t in range(PLANES):
            sq_out(t, 0)
            nc.sync.dma_start(sq_aside[:, t, :], sq_row[t][:, halves[0]])
        z_sum(1)
        h_product(1)
        for t in range(2):
            h_out(t, 0)
        for t in range(2, PLANES):
            nc.vector.tensor_copy(h_row[t][:, halves[0]], h_bank[t, 0][:])

        sq_n4 = sbuf("sq_n4", [P, PLANES, HALF], F32)
        h_n5 = {t: sbuf("h_n5_%d" % t, [P, HALF], F32) for t in (last - 1, last)}
        total = [sbuf("total%d" % c, [P, PLANES, HALF], F32) for c in range(2)]
        inv_root = [sbuf("inv_root%d" % c, [P, PLANES, HALF], F32) for c in range(2)]
        result = [sbuf("result%d" % c, [P, PLANES, HALF], F32) for c in range(2)]
        result_bf = [sbuf("result_bf%d" % c, [P, HALF, PLANES], BF16) for c in range(2)]
        out_codes = sbuf("out_codes", [P, S], U32)
        out_bytes = sbuf("out_bytes", [P, S], U8)
        out_rows = out_0.rearrange("(p t) j -> p t j", t=PLANES)

        def add_squares(t, c):
            if c == 0:
                other, own = looked_up(sq_row[t], n4_sb, halves[0]), sq_aside[:, t, :]
            else:
                other, own = sq_n4[:, t, :], sq_row[t][:, late]
            nc.vector.tensor_tensor(total[c][:, t, :], other, own, ALU.add)

        def root(t, c):
            nc.scalar.activation(
                inv_root[c][:, t, :], total[c][:, t, :], ACT.Abs_reciprocal_sqrt, bias=quarter[:]
            )

        def quotient(t, c):
            if c == 1 and t in h_n5:
                numerator = h_n5[t][:]
            else:
                numerator = looked_up(h_row[t], n5_sb, halves[c])
            nc.vector.tensor_tensor(result[c][:, t, :], numerator, inv_root[c][:, t, :], ALU.mult)
            nc.sync.dma_start(out_rows[:, t, halves[c]], result[c][:, t, :])

        def quantise_result(c):
            cols = halves[c]
            nc.vector.quantize_mx(
                out=out_codes[:, cols].bitcast(FP8X4), scales=out_bytes[:, cols],
                in_=result_bf[c][:].rearrange("p j t -> p (j t)"),
            )
            nc.sync.dma_start(as_words(out_1)[:, cols], out_codes[:, cols].bitcast(I32))

        steps = [(t, c) for c in range(2) for t in range(PLANES)]
        sq_out(0, 1)
        add_squares(0, 0)
        sq_out(1, 1)
        h_out(0, 1)
        for k, (t, c) in enumerate(steps[:-1]):
            root(t, c)
            add_squares(*steps[k + 1])
            if k + 1 < PLANES:
                h_out(k + 1, 1)
            if k + 2 < PLANES:
                sq_out(k + 2, 1)
            elif k + 2 < len(steps):
                ahead = k + 2 - PLANES
                fetch(sq_n4[:, ahead, :], sq_row[ahead], n4_sb, late)
            if c == 1 and t + 1 in h_n5:
                fetch(h_n5[t + 1][:], h_row[t + 1], n5_sb, late)
            quotient(t, c)
            if (t, c) == (last, 0):
                nc.vector.tensor_copy(woven(result_bf[0][:]), by_planes(result[0][:]))
            if (t, c) == (0, 1):
                quantise_result(0)
        root(*steps[-1])
        quotient(*steps[-1])
        cut = VECTOR_WEAVES
        nc.vector.tensor_copy(woven(result_bf[1][:, :cut, :]), by_planes(result[1][:, :, :cut]))
        nc.scalar.copy(woven(result_bf[1][:, cut:, :]), by_planes(result[1][:, :, cut:]))
        quantise_result(1)
        for q in range(4):
            queue = nc.scalar if q % 2 else nc.sync
            queue.dma_start(
                out_2[0, 4 * q : 4 * q + 4, :].bitcast(I32),
                out_bytes[32 * q : 32 * q + 4, :].bitcast(I32),
            )
